import numpy as np
import ml_dtypes


def mxq(x, axis, fmt="e4m3"):
    dtype, down = {"e4m3": (ml_dtypes.float8_e4m3fn, 7), "e5m2": (ml_dtypes.float8_e5m2, 14)}[fmt]
    v = np.moveaxis(np.asarray(x, np.float32).astype(ml_dtypes.bfloat16).astype(np.float64), axis, -1)
    blocks = v.reshape(v.shape[:-1] + (-1, 32))
    amax = np.abs(blocks).max(-1, keepdims=True)
    byte = np.maximum(np.where(amax > 0, np.frexp(amax)[1] - 1 + 127, 0) - down, 1)
    scale = np.exp2(byte - 127.0)
    codes = (blocks / scale).astype(np.float32).astype(dtype).astype(np.float64)
    return np.moveaxis((codes * scale).reshape(v.shape), -1, axis)


WIDE = False


def mx_kscale(k, group=512):
    if not WIDE:
        return np.ones(k)
    levels = np.array([18, -18])
    if group != 512:
        return np.exp2(np.random.permutation(np.resize(levels, k // group))).repeat(group)
    if k % 512:
        return np.exp2(np.random.permutation(np.resize(levels, k // 32))).repeat(32)
    a = np.empty((k // 512, 16))
    for p in range(k // 512):
        a[p, :8] = np.random.permutation(np.resize(levels, 8))
        for g in range(8):
            far = levels[np.abs(levels - a[p, g]) >= 10]
            a[p, g + 8] = far[np.random.randint(len(far))]
    return np.exp2(a.ravel()).repeat(32)


def f64(x):
    return np.asarray(x).astype(np.float64)


G, D, K, M, N = 4, 128, 512, 128, 512


def setup_inputs():
    n = np.random.standard_normal
    s = mx_kscale(D, 0)[:, None]
    u = mx_kscale(K)[:, None]
    return {
        "x": (n((G, D, N)) * s).astype(np.float32),
        "w1": (n((G, D, K)) / np.sqrt(D) / s).astype(np.float32),
        "hs": (np.random.uniform(0.5, 2.0, (G, K, 1)) * u).astype(np.float32),
        "w2": (n((G, K, M)) / np.sqrt(K) / u).astype(np.float32),
        "r": n((G, M, N)).astype(np.float32),
    }


def reference(x, w1, hs, w2, r):
    xq = mxq(f64(x), 1, "e4m3")
    h = mxq(f64(w1), 1, "e4m3").transpose(0, 2, 1) @ xq
    h = (np.maximum(h, 0.0)) * f64(hs)
    y = mxq(f64(w2), 1, "e4m3").transpose(0, 2, 1) @ mxq(h, 1, "e4m3")
    y = y + f64(r)
    return y

@@ -1,0 +1,217 @@
+from contextlib import ExitStack
+
+import concourse.mybir as mybir
+
+G, D, K, M, N = 4, 128, 512, 128, 512
+FLOPS = 2 * G * (D * K * N + K * M * N)
+
+F32 = mybir.dt.float32
+BF16 = mybir.dt.bfloat16
+U32 = mybir.dt.uint32
+U8 = mybir.dt.uint8
+FP8X4 = mybir.dt.float8_e4m3fn_x4
+ALU = mybir.AluOpType
+ACT = mybir.ActivationFunctionType
+
+P = 128
+PACK = 4
+ROWS = D // PACK
+CHUNK = 128
+HALF = 256
+RUN = 4
+
+
+def tile_rows_gmlp_relu_res_kernel(tc, x, w1, hs, w2, r, out):
+    nc = tc.nc
+
+    with ExitStack() as ctx:
+        sb = ctx.enter_context(tc.tile_pool(name="sb", bufs=1))
+        ps = ctx.enter_context(tc.psum_pool(name="ps", bufs=1))
+        ctx.enter_context(tc.manual_schedule())
+
+        def new(name, shape, dtype):
+            return sb.tile(shape, dtype, name=name, align_bytes=64)
+
+        def quantize(name, values, words):
+            codes = new(name + "_codes", [P, words], U32)
+            scales = new(name + "_scales", [P, words], U8)
+            nc.vector.quantize_mx(out=codes[:].bitcast(FP8X4), scales=scales[:], in_=values)
+            return codes, scales
+
+        def as_words(ap):
+            return ap.rearrange("p (c i) t -> p c t i", i=RUN)
+
+        def as_rows(ap):
+            return ap.rearrange("p t (c i) -> p c t i", i=RUN)
+
+        hs_sb = new("hs_sb", [P, G, 8], F32)
+        nc.scalar.dma_start(out=hs_sb[:, :, 0:PACK], in_=hs.rearrange("g (s t) o -> s g (t o)", t=PACK))
+        w1_raw = new("w1_raw", [P, PACK, K], F32)
+        nc.sync.dma_start(out=w1_raw[:], in_=w1.rearrange("g (p j) k -> (g p) j k", j=PACK))
+        x_rows = x.rearrange("g (p j) n -> (g p) j n", j=PACK)
+        x_raw = []
+        for h in range(2):
+            t = new("x_raw%d" % h, [P, PACK, HALF], F32)
+            nc.sync.dma_start(out=t[:], in_=x_rows[:, :, h * HALF:(h + 1) * HALF])
+            x_raw.append(t)
+        w2_rows = w2.rearrange("g (s t) m -> s g (t m)", t=PACK)
+        w2_raw = []
+        for q in range(2):
+            t = new("w2_raw%d" % q, [P, 2, PACK * M], F32)
+            nc.sync.dma_start(out=t[:], in_=w2_rows[:, 2 * q:2 * q + 2, :])
+            w2_raw.append(t)
+        r_rows = r.rearrange("g m n -> m g n")
+        r_sb = []
+        for q in range(2):
+            t = new("r_sb%d" % q, [P, 2, N], F32)
+            nc.sync.dma_start(out=t[:], in_=r_rows[:, 2 * q:2 * q + 2, :])
+            r_sb.append(t)
+        out_rows = out.rearrange("g m n -> m g n")
+
+        z_dve = [ps.tile([P, 512], F32, name="z_dve%d" % g) for g in range(2)]
+        z_act = [[ps.tile([P, 512], F32, name="z_act%d_%d" % (g, b)) for b in range(2)] for g in range(2)]
+        y_ps = [ps.tile([P, 512], F32, name="y_ps%d" % q) for q in range(2)]
+
+        hs_abs = new("hs_abs", [P, 2, PACK], F32)
+        hs_sign = new("hs_sign", [P, 2, PACK], F32)
+        nc.scalar.activation(out=hs_abs[:], in_=hs_sb[:, 2:4, 0:PACK], func=ACT.Abs)
+        nc.scalar.activation(out=hs_sign[:], in_=hs_sb[:, 2:4, 0:PACK], func=ACT.Sign)
+
+        w1_src = w1_raw[:].rearrange("p j (s t) -> p s j t", t=PACK)
+        w1_bf = [new("w1_bf%d" % u, [P, 2, P, PACK], BF16) for u in range(2)]
+        nc.vector.tensor_copy(out=w1_bf[0][:].rearrange("p t s j -> p s j t"), in_=w1_src[:, :, :, 0:2])
+        nc.scalar.copy(out=w1_bf[1][:].rearrange("p t s j -> p s j t"), in_=w1_src[:, :, :, 2:4])
+        w1_q = [quantize("w1_%d" % u, w1_bf[u][:].rearrange("p t s j -> p (t s j)"), 2 * P) for u in range(2)]
+
+        x_bf = [new("x_bf%d" % c, [P, CHUNK, PACK], BF16) for c in range(2)]
+        nc.scalar.copy(out=as_words(x_bf[0][:]), in_=as_rows(x_raw[0][:, :, 0:CHUNK]))
+        nc.vector.tensor_copy(out=as_words(x_bf[1][:]), in_=as_rows(x_raw[0][:, :, CHUNK:HALF]))
+        x_q = {}
+        for c in range(2):
+            codes, scales = quantize("x_%d" % c, x_bf[c][:].rearrange("p n j -> p (n j)"), CHUNK)
+            x_q[c] = (codes, scales, 0)
+
+        def first(g, t, c, dst):
+            rows = slice(ROWS * g, ROWS * (g + 1))
+            wc, wsc = w1_q[t // 2]
+            cols = slice(P * (t % 2), P * (t % 2 + 1))
+            xc, xsc, o = x_q[c]
+            nc.tensor.matmul_mx(
+                out=dst,
+                lhsT=wc[rows, cols].bitcast(FP8X4), lhsT_scale=wsc[rows, cols],
+                rhs=xc[rows, o:o + CHUNK].bitcast(FP8X4), rhs_scale=xsc[rows, o:o + CHUNK],
+                start=True, stop=True)
+
+        def first_round(c):
+            h, b = divmod(c, 2)
+            for k in range(4):
+                slot = slice(CHUNK * k, CHUNK * (k + 1))
+                for g in range(2):
+                    first(g, k, c, z_dve[g][:, slot])
+                cc, tt = divmod(k, 2)
+                aslot = slice(HALF * tt + CHUNK * cc, HALF * tt + CHUNK * (cc + 1))
+                for g in range(2):
+                    first(2 + g, 2 * b + tt, 2 * h + cc, z_act[g][b][:, aslot])
+
+        h_bf = [[new("h_bf%d_%d" % (q, h), [P, 2, HALF, PACK], BF16) for h in range(2)] for q in range(2)]
+        h_rows = [[new("h_rows%d_%d" % (g, h), [P, PACK, HALF], BF16) for h in range(2)] for g in range(2)]
+
+        def hidden_dve(c):
+            h, b = divmod(c, 2)
+            for g in range(2):
+                nc.vector.scalar_tensor_tensor(
+                    out=h_bf[0][h][:, g, CHUNK * b:CHUNK * (b + 1), :],
+                    in0=z_dve[g][:].rearrange("p (t n) -> p n t", t=PACK),
+                    scalar=0.0,
+                    in1=hs_sb[:, g, 0:PACK].unsqueeze(1).to_broadcast([P, CHUNK, PACK]),
+                    op0=ALU.max, op1=ALU.mult)
+
+        def hidden_act(c):
+            h, b = divmod(c, 2)
+            for g in range(2):
+                for tt in range(2):
+                    t = 2 * b + tt
+                    nc.scalar.activation(
+                        out=h_rows[g][h][:, t, :], in_=z_act[g][b][:, HALF * tt:HALF * (tt + 1)],
+                        func=ACT.Relu, scale=hs_abs[:, g, t:t + 1])
+
+        def interleave_h(copy, g, h):
+            copy(out=as_words(h_bf[1][h][:, g, :, :]), in_=as_rows(h_rows[g][h][:]))
+
+        def quantize_h(q, h):
+            return quantize("h_%d_%d" % (q, h), h_bf[q][h][:].rearrange("p g n t -> p (g n t)"), 2 * HALF)
+
+        w2_bf = [new("w2_bf%d" % q, [P, 2, M, PACK], BF16) for q in range(2)]
+
+        def signed_w2(g):
+            nc.vector.tensor_tensor(
+                out=as_words(w2_bf[1][:, g, :, :]),
+                in0=as_rows(w2_raw[1][:, g, :].rearrange("p (t m) -> p t m", t=PACK)),
+                in1=hs_sign[:, g, :].unsqueeze(1).unsqueeze(3).to_broadcast([P, M // RUN, PACK, RUN]),
+                op=ALU.mult)
+
+        def quantize_w2(q):
+            return quantize("w2_%d" % q, w2_bf[q][:].rearrange("p g m t -> p (g m t)"), 2 * M)
+
+        def second(q, w2_q, h_q):
+            for g in range(2):
+                for b in range(2):
+                    cols = slice(HALF * g + CHUNK * b, HALF * g + CHUNK * (b + 1))
+                    nc.tensor.matmul_mx(
+                        out=y_ps[q][:, cols],
+                        lhsT=w2_q[0][:, M * g:M * (g + 1)].bitcast(FP8X4), lhsT_scale=w2_q[1][:, M * g:M * (g + 1)],
+                        rhs=h_q[0][:, cols].bitcast(FP8X4), rhs_scale=h_q[1][:, cols],
+                        start=True, stop=True)
+
+        def finish(q, h, g0, g1):
+            res = new("res%d_%d_%d" % (q, h, g0), [P, g1 - g0, HALF], F32)
+            cols = slice(HALF * h, HALF * (h + 1))
+            nc.vector.tensor_tensor(
+                out=res[:], in0=y_ps[q][:].rearrange("p (g n) -> p g n", g=2)[:, g0:g1, :],
+                in1=r_sb[q][:, g0:g1, cols], op=ALU.add)
+            nc.sync.dma_start(out=out_rows[:, 2 * q + g0:2 * q + g1, cols], in_=res[:])
+
+        first_round(0)
+        x_bf1 = new("x_bf_h1", [P, HALF, PACK], BF16)
+        nc.vector.tensor_copy(out=as_words(x_bf1[:]), in_=as_rows(x_raw[1][:]))
+        hidden_dve(0)
+        hidden_act(0)
+        codes, scales = quantize("x_h1", x_bf1[:].rearrange("p n j -> p (n j)"), HALF)
+        x_q[2] = (codes, scales, 0)
+        x_q[3] = (codes, scales, CHUNK)
+
+        first_round(1)
+        nc.scalar.copy(
+            out=w2_bf[0][:].rearrange("p g (c i) t -> p g c t i", i=RUN),
+            in_=w2_raw[0][:].rearrange("p g (t c i) -> p g c t i", t=PACK, i=RUN))
+        signed_w2(0)
+        hidden_dve(1)
+        hidden_act(1)
+
+        first_round(2)
+        w2_q0 = quantize_w2(0)
+        h_q = quantize_h(0, 0)
+        signed_w2(1)
+        second(0, w2_q0, h_q)
+        interleave_h(nc.scalar.copy, 0, 0)
+        interleave_h(nc.scalar.copy, 1, 0)
+        hidden_dve(2)
+        hidden_act(2)
+
+        first_round(3)
+        w2_q1 = quantize_w2(1)
+        finish(0, 0, 0, 2)
+        h_q = quantize_h(1, 0)
+        second(1, w2_q1, h_q)
+        hidden_dve(3)
+        hidden_act(3)
+        finish(1, 0, 0, 2)
+        h_q = quantize_h(0, 1)
+        second(0, w2_q0, h_q)
+        interleave_h(nc.scalar.copy, 0, 1)
+        interleave_h(nc.vector.tensor_copy, 1, 1)
+        h_q = quantize_h(1, 1)
+        second(1, w2_q1, h_q)
+        finish(0, 1, 0, 2)
+        finish(1, 1, 0, 1)
+        finish(1, 1, 1, 2)

@@ -102,44 +102,38 @@ def tile_rows_gmlp_relu_res_kernel(tc, x, w1, hs, w2, r, out):
                 rhs=xc[rows, o:o + CHUNK].bitcast(FP8X4), rhs_scale=xsc[rows, o:o + CHUNK],
                 start=True, stop=True)
 
-        def first_round(c):
+        def step(c, g):
             h, b = divmod(c, 2)
             for k in range(4):
-                slot = slice(CHUNK * k, CHUNK * (k + 1))
-                for g in range(2):
-                    first(g, k, c, z_dve[g][:, slot])
+                first(g, k, c, z_dve[g][:, CHUNK * k:CHUNK * (k + 1)])
                 cc, tt = divmod(k, 2)
-                aslot = slice(HALF * tt + CHUNK * cc, HALF * tt + CHUNK * (cc + 1))
-                for g in range(2):
-                    first(2 + g, 2 * b + tt, 2 * h + cc, z_act[g][b][:, aslot])
+                first(2 + g, 2 * b + tt, 2 * h + cc, z_act[g][b][:, HALF * tt + CHUNK * cc:HALF * tt + CHUNK * (cc + 1)])
 
         h_bf = [[new("h_bf%d_%d" % (q, h), [P, 2, HALF, PACK], BF16) for h in range(2)] for q in range(2)]
         h_rows = [[new("h_rows%d_%d" % (g, h), [P, PACK, HALF], BF16) for h in range(2)] for g in range(2)]
 
-        def hidden_dve(c):
+        def hidden_dve(c, g):
             h, b = divmod(c, 2)
-            for g in range(2):
-                nc.vector.scalar_tensor_tensor(
-                    out=h_bf[0][h][:, g, CHUNK * b:CHUNK * (b + 1), :],
-                    in0=z_dve[g][:].rearrange("p (t n) -> p n t", t=PACK),
-                    scalar=0.0,
-                    in1=hs_sb[:, g, 0:PACK].unsqueeze(1).to_broadcast([P, CHUNK, PACK]),
-                    op0=ALU.max, op1=ALU.mult)
+            nc.vector.scalar_tensor_tensor(
+                out=h_bf[0][h][:, g, CHUNK * b:CHUNK * (b + 1), :],
+                in0=z_dve[g][:].rearrange("p (t n) -> p n t", t=PACK),
+                scalar=0.0,
+                in1=hs_sb[:, g, 0:PACK].unsqueeze(1).to_broadcast([P, CHUNK, PACK]),
+                op0=ALU.max, op1=ALU.mult)
 
-        def hidden_act(c):
+        def hidden_act(c, g):
             h, b = divmod(c, 2)
-            for g in range(2):
-                for tt in range(2):
-                    t = 2 * b + tt
-                    nc.scalar.activation(
-                        out=h_rows[g][h][:, t, :], in_=z_act[g][b][:, HALF * tt:HALF * (tt + 1)],
-                        func=ACT.Relu, scale=hs_abs[:, g, t:t + 1])
+            for tt in range(2):
+                t = 2 * b + tt
+                nc.scalar.activation(
+                    out=h_rows[g][h][:, t, :], in_=z_act[g][b][:, HALF * tt:HALF * (tt + 1)],
+                    func=ACT.Relu, scale=hs_abs[:, g, t:t + 1])
 
         def interleave_h(copy, g, h):
             copy(out=as_words(h_bf[1][h][:, g, :, :]), in_=as_rows(h_rows[g][h][:]))
 
-        def quantize_h(q, h):
-            return quantize("h_%d_%d" % (q, h), h_bf[q][h][:].rearrange("p g n t -> p (g n t)"), 2 * HALF)
+        def quantize_h(q, h, g0, g1):
+            return quantize("h_%d_%d_%d" % (q, h, g0), h_bf[q][h][:, g0:g1, :, :].rearrange("p g n t -> p (g n t)"), (g1 - g0) * HALF)
 
         w2_bf = [new("w2_bf%d" % q, [P, 2, M, PACK], BF16) for q in range(2)]
 
@@ -153,65 +147,78 @@ def tile_rows_gmlp_relu_res_kernel(tc, x, w1, hs, w2, r, out):
         def quantize_w2(q):
             return quantize("w2_%d" % q, w2_bf[q][:].rearrange("p g m t -> p (g m t)"), 2 * M)
 
-        def second(q, w2_q, h_q):
-            for g in range(2):
+        def second(bank, w2_q, h_q, g0, g1):
+            for g in range(g0, g1):
                 for b in range(2):
-                    cols = slice(HALF * g + CHUNK * b, HALF * g + CHUNK * (b + 1))
+                    cols = slice(HALF * (g - g0) + CHUNK * b, HALF * (g - g0) + CHUNK * (b + 1))
                     nc.tensor.matmul_mx(
-                        out=y_ps[q][:, cols],
+                        out=y_ps[bank][:, cols],
                         lhsT=w2_q[0][:, M * g:M * (g + 1)].bitcast(FP8X4), lhsT_scale=w2_q[1][:, M * g:M * (g + 1)],
                         rhs=h_q[0][:, cols].bitcast(FP8X4), rhs_scale=h_q[1][:, cols],
                         start=True, stop=True)
 
-        def finish(q, h, g0, g1):
+        def finish(bank, q, h, g0, g1):
             res = new("res%d_%d_%d" % (q, h, g0), [P, g1 - g0, HALF], F32)
             cols = slice(HALF * h, HALF * (h + 1))
             nc.vector.tensor_tensor(
-                out=res[:], in0=y_ps[q][:].rearrange("p (g n) -> p g n", g=2)[:, g0:g1, :],
+                out=res[:], in0=y_ps[bank][:, 0:HALF * (g1 - g0)].rearrange("p (g n) -> p g n", n=HALF),
                 in1=r_sb[q][:, g0:g1, cols], op=ALU.add)
             nc.sync.dma_start(out=out_rows[:, 2 * q + g0:2 * q + g1, cols], in_=res[:])
 
-        first_round(0)
+        step(0, 0)
+        step(0, 1)
         x_bf1 = new("x_bf_h1", [P, HALF, PACK], BF16)
-        nc.vector.tensor_copy(out=as_words(x_bf1[:]), in_=as_rows(x_raw[1][:]))
-        hidden_dve(0)
-        hidden_act(0)
+        nc.scalar.copy(out=as_words(x_bf1[:, 0:CHUNK, :]), in_=as_rows(x_raw[1][:, :, 0:CHUNK]))
+        nc.vector.tensor_copy(out=as_words(x_bf1[:, CHUNK:HALF, :]), in_=as_rows(x_raw[1][:, :, CHUNK:HALF]))
         codes, scales = quantize("x_h1", x_bf1[:].rearrange("p n j -> p (n j)"), HALF)
         x_q[2] = (codes, scales, 0)
         x_q[3] = (codes, scales, CHUNK)
 
-        first_round(1)
+        hidden_dve(0, 0)
+        hidden_act(0, 0)
+        step(1, 0)
         nc.scalar.copy(
             out=w2_bf[0][:].rearrange("p g (c i) t -> p g c t i", i=RUN),
             in_=w2_raw[0][:].rearrange("p g (t c i) -> p g c t i", t=PACK, i=RUN))
+        hidden_dve(0, 1)
+        hidden_act(0, 1)
+        step(1, 1)
         signed_w2(0)
-        hidden_dve(1)
-        hidden_act(1)
-
-        first_round(2)
-        w2_q0 = quantize_w2(0)
-        h_q = quantize_h(0, 0)
+        hidden_dve(1, 0)
+        hidden_act(1, 0)
+        step(2, 0)
         signed_w2(1)
-        second(0, w2_q0, h_q)
+        hidden_dve(1, 1)
+        hidden_act(1, 1)
+        step(2, 1)
+        w2_q0 = quantize_w2(0)
+        h_q = quantize_h(0, 0, 0, 2)
         interleave_h(nc.scalar.copy, 0, 0)
         interleave_h(nc.scalar.copy, 1, 0)
-        hidden_dve(2)
-        hidden_act(2)
-
-        first_round(3)
+        hidden_dve(2, 0)
+        second(0, w2_q0, h_q, 0, 2)
+        step(3, 0)
         w2_q1 = quantize_w2(1)
-        finish(0, 0, 0, 2)
-        h_q = quantize_h(1, 0)
-        second(1, w2_q1, h_q)
-        hidden_dve(3)
-        hidden_act(3)
-        finish(1, 0, 0, 2)
-        h_q = quantize_h(0, 1)
-        second(0, w2_q0, h_q)
+        hidden_dve(2, 1)
+        hidden_act(2, 0)
+        hidden_act(2, 1)
+        step(3, 1)
+        finish(0, 0, 0, 0, 2)
+        h_q = quantize_h(1, 0, 0, 2)
+        hidden_dve(3, 0)
+        second(1, w2_q1, h_q, 0, 2)
+        hidden_dve(3, 1)
+        hidden_act(3, 0)
+        hidden_act(3, 1)
+        finish(1, 1, 0, 0, 2)
+        h_q = quantize_h(0, 1, 0, 2)
+        second(0, w2_q0, h_q, 0, 2)
         interleave_h(nc.scalar.copy, 0, 1)
-        interleave_h(nc.vector.tensor_copy, 1, 1)
-        h_q = quantize_h(1, 1)
-        second(1, w2_q1, h_q)
-        finish(0, 1, 0, 2)
-        finish(1, 1, 0, 1)
-        finish(1, 1, 1, 2)
+        interleave_h(nc.scalar.copy, 1, 1)
+        h_q = quantize_h(1, 1, 0, 1)
+        second(1, w2_q1, h_q, 0, 1)
+        finish(0, 0, 1, 0, 2)
+        h_q = quantize_h(1, 1, 1, 2)
+        second(0, w2_q1, h_q, 1, 2)
+        finish(1, 1, 1, 0, 1)
+        finish(0, 1, 1, 1, 2)

@@ -45,7 +45,6 @@ def tile_rows_gmlp_relu_res_kernel(tc, x, w1, hs, w2, r, out):
             return ap.rearrange("p t (c i) -> p c t i", i=RUN)
 
         hs_sb = new("hs_sb", [P, G, 8], F32)
-        nc.scalar.dma_start(out=hs_sb[:, :, 0:PACK], in_=hs.rearrange("g (s t) o -> s g (t o)", t=PACK))
         w1_raw = new("w1_raw", [P, PACK, K], F32)
         nc.sync.dma_start(out=w1_raw[:], in_=w1.rearrange("g (p j) k -> (g p) j k", j=PACK))
         x_rows = x.rearrange("g (p j) n -> (g p) j n", j=PACK)
@@ -54,6 +53,8 @@ def tile_rows_gmlp_relu_res_kernel(tc, x, w1, hs, w2, r, out):
             t = new("x_raw%d" % h, [P, PACK, HALF], F32)
             nc.sync.dma_start(out=t[:], in_=x_rows[:, :, h * HALF:(h + 1) * HALF])
             x_raw.append(t)
+            if h == 0:
+                nc.sync.dma_start(out=hs_sb[:, :, 0:PACK], in_=hs.rearrange("g (s t) o -> s g (t o)", t=PACK))
         w2_rows = w2.rearrange("g (s t) m -> s g (t m)", t=PACK)
         w2_raw = []
         for q in range(2):
@@ -73,9 +74,7 @@ def tile_rows_gmlp_relu_res_kernel(tc, x, w1, hs, w2, r, out):
         y_ps = [ps.tile([P, 512], F32, name="y_ps%d" % q) for q in range(2)]
 
         hs_abs = new("hs_abs", [P, 2, PACK], F32)
-        hs_sign = new("hs_sign", [P, 2, PACK], F32)
-        nc.scalar.activation(out=hs_abs[:], in_=hs_sb[:, 2:4, 0:PACK], func=ACT.Abs)
-        nc.scalar.activation(out=hs_sign[:], in_=hs_sb[:, 2:4, 0:PACK], func=ACT.Sign)
+        hs_sign = new("hs_sign", [P, 2, PACK], BF16)
 
         w1_src = w1_raw[:].rearrange("p j (s t) -> p s j t", t=PACK)
         w1_bf = [new("w1_bf%d" % u, [P, 2, P, PACK], BF16) for u in range(2)]
@@ -86,6 +85,8 @@ def tile_rows_gmlp_relu_res_kernel(tc, x, w1, hs, w2, r, out):
         x_bf = [new("x_bf%d" % c, [P, CHUNK, PACK], BF16) for c in range(2)]
         nc.scalar.copy(out=as_words(x_bf[0][:]), in_=as_rows(x_raw[0][:, :, 0:CHUNK]))
         nc.vector.tensor_copy(out=as_words(x_bf[1][:]), in_=as_rows(x_raw[0][:, :, CHUNK:HALF]))
+        nc.scalar.activation(out=hs_abs[:], in_=hs_sb[:, 2:4, 0:PACK], func=ACT.Abs)
+        nc.scalar.activation(out=hs_sign[:], in_=hs_sb[:, 2:4, 0:PACK], func=ACT.Sign)
         x_q = {}
         for c in range(2):
             codes, scales = quantize("x_%d" % c, x_bf[c][:].rearrange("p n j -> p (n j)"), CHUNK)
@@ -137,12 +138,16 @@ def tile_rows_gmlp_relu_res_kernel(tc, x, w1, hs, w2, r, out):
 
         w2_bf = [new("w2_bf%d" % q, [P, 2, M, PACK], BF16) for q in range(2)]
 
-        def signed_w2(g):
+        w2_plain = new("w2_plain", [P, 2, M, PACK], BF16)
+
+        def interleave_w2(copy, dst, q):
+            copy(out=dst[:].rearrange("p g (c i) t -> p g c t i", i=RUN),
+                 in_=w2_raw[q][:].rearrange("p g (t c i) -> p g c t i", t=PACK, i=RUN))
+
+        def signed_w2():
             nc.vector.tensor_tensor(
-                out=as_words(w2_bf[1][:, g, :, :]),
-                in0=as_rows(w2_raw[1][:, g, :].rearrange("p (t m) -> p t m", t=PACK)),
-                in1=hs_sign[:, g, :].unsqueeze(1).unsqueeze(3).to_broadcast([P, M // RUN, PACK, RUN]),
-                op=ALU.mult)
+                out=w2_bf[1][:], in0=w2_plain[:],
+                in1=hs_sign[:].unsqueeze(2).to_broadcast([P, 2, M, PACK]), op=ALU.mult)
 
         def quantize_w2(q):
             return quantize("w2_%d" % q, w2_bf[q][:].rearrange("p g m t -> p (g m t)"), 2 * M)
@@ -170,24 +175,21 @@ def tile_rows_gmlp_relu_res_kernel(tc, x, w1, hs, w2, r, out):
         x_bf1 = new("x_bf_h1", [P, HALF, PACK], BF16)
         nc.scalar.copy(out=as_words(x_bf1[:, 0:CHUNK, :]), in_=as_rows(x_raw[1][:, :, 0:CHUNK]))
         nc.vector.tensor_copy(out=as_words(x_bf1[:, CHUNK:HALF, :]), in_=as_rows(x_raw[1][:, :, CHUNK:HALF]))
-        codes, scales = quantize("x_h1", x_bf1[:].rearrange("p n j -> p (n j)"), HALF)
-        x_q[2] = (codes, scales, 0)
-        x_q[3] = (codes, scales, CHUNK)
-
         hidden_dve(0, 0)
         hidden_act(0, 0)
         step(1, 0)
-        nc.scalar.copy(
-            out=w2_bf[0][:].rearrange("p g (c i) t -> p g c t i", i=RUN),
-            in_=w2_raw[0][:].rearrange("p g (t c i) -> p g c t i", t=PACK, i=RUN))
+        codes, scales = quantize("x_h1", x_bf1[:].rearrange("p n j -> p (n j)"), HALF)
+        x_q[2] = (codes, scales, 0)
+        x_q[3] = (codes, scales, CHUNK)
         hidden_dve(0, 1)
         hidden_act(0, 1)
         step(1, 1)
-        signed_w2(0)
+        interleave_w2(nc.scalar.copy, w2_bf[0], 0)
+        interleave_w2(nc.vector.tensor_copy, w2_plain, 1)
         hidden_dve(1, 0)
         hidden_act(1, 0)
         step(2, 0)
-        signed_w2(1)
+        signed_w2()
         hidden_dve(1, 1)
         hidden_act(1, 1)
         step(2, 1)
@@ -210,15 +212,18 @@ def tile_rows_gmlp_relu_res_kernel(tc, x, w1, hs, w2, r, out):
         hidden_dve(3, 1)
         hidden_act(3, 0)
         hidden_act(3, 1)
+        h_q = quantize_h(0, 1, 0, 1)
+        second(0, w2_q0, h_q, 0, 1)
         finish(1, 1, 0, 0, 2)
-        h_q = quantize_h(0, 1, 0, 2)
-        second(0, w2_q0, h_q, 0, 2)
+        h_q = quantize_h(0, 1, 1, 2)
+        second(1, w2_q0, h_q, 1, 2)
         interleave_h(nc.scalar.copy, 0, 1)
         interleave_h(nc.scalar.copy, 1, 1)
         h_q = quantize_h(1, 1, 0, 1)
-        second(1, w2_q1, h_q, 0, 1)
-        finish(0, 0, 1, 0, 2)
+        finish(0, 0, 1, 0, 1)
+        second(0, w2_q1, h_q, 0, 1)
+        finish(1, 0, 1, 1, 2)
         h_q = quantize_h(1, 1, 1, 2)
-        second(0, w2_q1, h_q, 1, 2)
-        finish(1, 1, 1, 0, 1)
-        finish(0, 1, 1, 1, 2)
+        second(1, w2_q1, h_q, 1, 2)
+        finish(0, 1, 1, 0, 1)
+        finish(1, 1, 1, 1, 2)

@@ -53,14 +53,14 @@ def tile_rows_gmlp_relu_res_kernel(tc, x, w1, hs, w2, r, out):
             t = new("x_raw%d" % h, [P, PACK, HALF], F32)
             nc.sync.dma_start(out=t[:], in_=x_rows[:, :, h * HALF:(h + 1) * HALF])
             x_raw.append(t)
-            if h == 0:
+            if h == 1:
                 nc.sync.dma_start(out=hs_sb[:, :, 0:PACK], in_=hs.rearrange("g (s t) o -> s g (t o)", t=PACK))
         w2_rows = w2.rearrange("g (s t) m -> s g (t m)", t=PACK)
-        w2_raw = []
-        for q in range(2):
+        w2_raw = {}
+        for q in (1, 0):
             t = new("w2_raw%d" % q, [P, 2, PACK * M], F32)
             nc.sync.dma_start(out=t[:], in_=w2_rows[:, 2 * q:2 * q + 2, :])
-            w2_raw.append(t)
+            w2_raw[q] = t
         r_rows = r.rearrange("g m n -> m g n")
         r_sb = []
         for q in range(2):
@@ -85,8 +85,6 @@ def tile_rows_gmlp_relu_res_kernel(tc, x, w1, hs, w2, r, out):
         x_bf = [new("x_bf%d" % c, [P, CHUNK, PACK], BF16) for c in range(2)]
         nc.scalar.copy(out=as_words(x_bf[0][:]), in_=as_rows(x_raw[0][:, :, 0:CHUNK]))
         nc.vector.tensor_copy(out=as_words(x_bf[1][:]), in_=as_rows(x_raw[0][:, :, CHUNK:HALF]))
-        nc.scalar.activation(out=hs_abs[:], in_=hs_sb[:, 2:4, 0:PACK], func=ACT.Abs)
-        nc.scalar.activation(out=hs_sign[:], in_=hs_sb[:, 2:4, 0:PACK], func=ACT.Sign)
         x_q = {}
         for c in range(2):
             codes, scales = quantize("x_%d" % c, x_bf[c][:].rearrange("p n j -> p (n j)"), CHUNK)
@@ -136,29 +134,34 @@ def tile_rows_gmlp_relu_res_kernel(tc, x, w1, hs, w2, r, out):
         def quantize_h(q, h, g0, g1):
             return quantize("h_%d_%d_%d" % (q, h, g0), h_bf[q][h][:, g0:g1, :, :].rearrange("p g n t -> p (g n t)"), (g1 - g0) * HALF)
 
-        w2_bf = [new("w2_bf%d" % q, [P, 2, M, PACK], BF16) for q in range(2)]
+        w2_bf = new("w2_bf", [P, G, M, PACK], BF16)
+
+        def w2_rows_of(g):
+            return w2_raw[g // 2][:, g % 2, :].rearrange("p (t m) -> p t m", t=PACK)
+
+        def interleave_w2(copy, g):
+            copy(out=as_words(w2_bf[:, g, :, :]), in_=as_rows(w2_rows_of(g)))
 
         w2_plain = new("w2_plain", [P, 2, M, PACK], BF16)
 
-        def interleave_w2(copy, dst, q):
-            copy(out=dst[:].rearrange("p g (c i) t -> p g c t i", i=RUN),
-                 in_=w2_raw[q][:].rearrange("p g (t c i) -> p g c t i", t=PACK, i=RUN))
+        def interleave_w2_pool(dst, g):
+            nc.gpsimd.tensor_scalar(
+                out=dst, in0=w2_rows_of(g).rearrange("p t m -> p m t"),
+                scalar1=1.0, scalar2=0.0, op0=ALU.mult, op1=ALU.add)
 
         def signed_w2():
             nc.vector.tensor_tensor(
-                out=w2_bf[1][:], in0=w2_plain[:],
+                out=w2_bf[:, 2:4, :, :], in0=w2_plain[:],
                 in1=hs_sign[:].unsqueeze(2).to_broadcast([P, 2, M, PACK]), op=ALU.mult)
 
-        def quantize_w2(q):
-            return quantize("w2_%d" % q, w2_bf[q][:].rearrange("p g m t -> p (g m t)"), 2 * M)
-
-        def second(bank, w2_q, h_q, g0, g1):
+        def second(bank, q, h_q, g0, g1):
             for g in range(g0, g1):
                 for b in range(2):
                     cols = slice(HALF * (g - g0) + CHUNK * b, HALF * (g - g0) + CHUNK * (b + 1))
                     nc.tensor.matmul_mx(
                         out=y_ps[bank][:, cols],
-                        lhsT=w2_q[0][:, M * g:M * (g + 1)].bitcast(FP8X4), lhsT_scale=w2_q[1][:, M * g:M * (g + 1)],
+                        lhsT=w2_q[0][:, M * (2 * q + g):M * (2 * q + g + 1)].bitcast(FP8X4),
+                        lhsT_scale=w2_q[1][:, M * (2 * q + g):M * (2 * q + g + 1)],
                         rhs=h_q[0][:, cols].bitcast(FP8X4), rhs_scale=h_q[1][:, cols],
                         start=True, stop=True)
 
@@ -175,32 +178,35 @@ def tile_rows_gmlp_relu_res_kernel(tc, x, w1, hs, w2, r, out):
         x_bf1 = new("x_bf_h1", [P, HALF, PACK], BF16)
         nc.scalar.copy(out=as_words(x_bf1[:, 0:CHUNK, :]), in_=as_rows(x_raw[1][:, :, 0:CHUNK]))
         nc.vector.tensor_copy(out=as_words(x_bf1[:, CHUNK:HALF, :]), in_=as_rows(x_raw[1][:, :, CHUNK:HALF]))
-        hidden_dve(0, 0)
-        hidden_act(0, 0)
-        step(1, 0)
+        nc.scalar.activation(out=hs_abs[:], in_=hs_sb[:, 2:4, 0:PACK], func=ACT.Abs)
+        nc.scalar.activation(out=hs_sign[:], in_=hs_sb[:, 2:4, 0:PACK], func=ACT.Sign)
         codes, scales = quantize("x_h1", x_bf1[:].rearrange("p n j -> p (n j)"), HALF)
         x_q[2] = (codes, scales, 0)
         x_q[3] = (codes, scales, CHUNK)
+        interleave_w2_pool(w2_plain[:, 0, :, :], 2)
+        interleave_w2_pool(w2_plain[:, 1, :, :], 3)
+        interleave_w2_pool(w2_bf[:, 1, :, :], 1)
+        hidden_dve(0, 0)
+        hidden_act(0, 0)
+        step(1, 0)
         hidden_dve(0, 1)
         hidden_act(0, 1)
         step(1, 1)
-        interleave_w2(nc.scalar.copy, w2_bf[0], 0)
-        interleave_w2(nc.vector.tensor_copy, w2_plain, 1)
+        interleave_w2(nc.scalar.copy, 0)
         hidden_dve(1, 0)
         hidden_act(1, 0)
         step(2, 0)
-        signed_w2()
         hidden_dve(1, 1)
         hidden_act(1, 1)
         step(2, 1)
-        w2_q0 = quantize_w2(0)
+        signed_w2()
         h_q = quantize_h(0, 0, 0, 2)
+        w2_q = quantize("w2", w2_bf[:].rearrange("p g m t -> p (g m t)"), G * M)
         interleave_h(nc.scalar.copy, 0, 0)
         interleave_h(nc.scalar.copy, 1, 0)
         hidden_dve(2, 0)
-        second(0, w2_q0, h_q, 0, 2)
+        second(0, 0, h_q, 0, 2)
         step(3, 0)
-        w2_q1 = quantize_w2(1)
         hidden_dve(2, 1)
         hidden_act(2, 0)
         hidden_act(2, 1)
@@ -208,22 +214,22 @@ def tile_rows_gmlp_relu_res_kernel(tc, x, w1, hs, w2, r, out):
         finish(0, 0, 0, 0, 2)
         h_q = quantize_h(1, 0, 0, 2)
         hidden_dve(3, 0)
-        second(1, w2_q1, h_q, 0, 2)
+        second(1, 1, h_q, 0, 2)
         hidden_dve(3, 1)
         hidden_act(3, 0)
         hidden_act(3, 1)
         h_q = quantize_h(0, 1, 0, 1)
-        second(0, w2_q0, h_q, 0, 1)
+        second(0, 0, h_q, 0, 1)
         finish(1, 1, 0, 0, 2)
         h_q = quantize_h(0, 1, 1, 2)
-        second(1, w2_q0, h_q, 1, 2)
+        second(1, 0, h_q, 1, 2)
         interleave_h(nc.scalar.copy, 0, 1)
         interleave_h(nc.scalar.copy, 1, 1)
         h_q = quantize_h(1, 1, 0, 1)
         finish(0, 0, 1, 0, 1)
-        second(0, w2_q1, h_q, 0, 1)
+        second(0, 1, h_q, 0, 1)
         finish(1, 0, 1, 1, 2)
         h_q = quantize_h(1, 1, 1, 2)
-        second(1, w2_q1, h_q, 1, 2)
+        second(1, 1, h_q, 1, 2)
         finish(0, 1, 1, 0, 1)
         finish(1, 1, 1, 1, 2)

from contextlib import ExitStack

import concourse.mybir as mybir

G, D, K, M, N = 4, 128, 512, 128, 512
FLOPS = 2 * G * (D * K * N + K * M * N)

F32 = mybir.dt.float32
BF16 = mybir.dt.bfloat16
U32 = mybir.dt.uint32
U8 = mybir.dt.uint8
FP8X4 = mybir.dt.float8_e4m3fn_x4
ALU = mybir.AluOpType
ACT = mybir.ActivationFunctionType

P = 128
PACK = 4
ROWS = D // PACK
CHUNK = 128
HALF = 256
RUN = 4


def tile_rows_gmlp_relu_res_kernel(tc, x, w1, hs, w2, r, out):
    nc = tc.nc

    with ExitStack() as ctx:
        sb = ctx.enter_context(tc.tile_pool(name="sb", bufs=1))
        ps = ctx.enter_context(tc.psum_pool(name="ps", bufs=1))
        ctx.enter_context(tc.manual_schedule())

        def new(name, shape, dtype):
            return sb.tile(shape, dtype, name=name, align_bytes=64)

        def quantize(name, values, words):
            codes = new(name + "_codes", [P, words], U32)
            scales = new(name + "_scales", [P, words], U8)
            nc.vector.quantize_mx(out=codes[:].bitcast(FP8X4), scales=scales[:], in_=values)
            return codes, scales

        def as_words(ap):
            return ap.rearrange("p (c i) t -> p c t i", i=RUN)

        def as_rows(ap):
            return ap.rearrange("p t (c i) -> p c t i", i=RUN)

        hs_sb = new("hs_sb", [P, G, 8], F32)
        w1_raw = new("w1_raw", [P, PACK, K], F32)
        nc.sync.dma_start(out=w1_raw[:], in_=w1.rearrange("g (p j) k -> (g p) j k", j=PACK))
        x_rows = x.rearrange("g (p j) n -> (g p) j n", j=PACK)
        x_raw = []
        for h in range(2):
            t = new("x_raw%d" % h, [P, PACK, HALF], F32)
            nc.sync.dma_start(out=t[:], in_=x_rows[:, :, h * HALF:(h + 1) * HALF])
            x_raw.append(t)
            if h == 1:
                nc.sync.dma_start(out=hs_sb[:, :, 0:PACK], in_=hs.rearrange("g (s t) o -> s g (t o)", t=PACK))
        w2_rows = w2.rearrange("g (s t) m -> s g (t m)", t=PACK)
        w2_raw = {}
        for q in (1, 0):
            t = new("w2_raw%d" % q, [P, 2, PACK * M], F32)
            nc.sync.dma_start(out=t[:], in_=w2_rows[:, 2 * q:2 * q + 2, :])
            w2_raw[q] = t
        r_rows = r.rearrange("g m n -> m g n")
        r_sb = []
        for q in range(2):
            t = new("r_sb%d" % q, [P, 2, N], F32)
            nc.sync.dma_start(out=t[:], in_=r_rows[:, 2 * q:2 * q + 2, :])
            r_sb.append(t)
        out_rows = out.rearrange("g m n -> m g n")

        z_dve = [ps.tile([P, 512], F32, name="z_dve%d" % g) for g in range(2)]
        z_act = [[ps.tile([P, 512], F32, name="z_act%d_%d" % (g, b)) for b in range(2)] for g in range(2)]
        y_ps = [ps.tile([P, 512], F32, name="y_ps%d" % q) for q in range(2)]

        hs_abs = new("hs_abs", [P, 2, PACK], F32)
        hs_sign = new("hs_sign", [P, 2, PACK], BF16)

        w1_src = w1_raw[:].rearrange("p j (s t) -> p s j t", t=PACK)
        w1_bf = [new("w1_bf%d" % u, [P, 2, P, PACK], BF16) for u in range(2)]
        nc.vector.tensor_copy(out=w1_bf[0][:].rearrange("p t s j -> p s j t"), in_=w1_src[:, :, :, 0:2])
        nc.scalar.copy(out=w1_bf[1][:].rearrange("p t s j -> p s j t"), in_=w1_src[:, :, :, 2:4])
        w1_q = [quantize("w1_%d" % u, w1_bf[u][:].rearrange("p t s j -> p (t s j)"), 2 * P) for u in range(2)]

        x_bf = [new("x_bf%d" % c, [P, CHUNK, PACK], BF16) for c in range(2)]
        nc.scalar.copy(out=as_words(x_bf[0][:]), in_=as_rows(x_raw[0][:, :, 0:CHUNK]))
        nc.vector.tensor_copy(out=as_words(x_bf[1][:]), in_=as_rows(x_raw[0][:, :, CHUNK:HALF]))
        x_q = {}
        for c in range(2):
            codes, scales = quantize("x_%d" % c, x_bf[c][:].rearrange("p n j -> p (n j)"), CHUNK)
            x_q[c] = (codes, scales, 0)

        def first(g, t, c, dst):
            rows = slice(ROWS * g, ROWS * (g + 1))
            wc, wsc = w1_q[t // 2]
            cols = slice(P * (t % 2), P * (t % 2 + 1))
            xc, xsc, o = x_q[c]
            nc.tensor.matmul_mx(
                out=dst,
                lhsT=wc[rows, cols].bitcast(FP8X4), lhsT_scale=wsc[rows, cols],
                rhs=xc[rows, o:o + CHUNK].bitcast(FP8X4), rhs_scale=xsc[rows, o:o + CHUNK],
                start=True, stop=True)

        def step(c, g):
            h, b = divmod(c, 2)
            for k in range(4):
                first(g, k, c, z_dve[g][:, CHUNK * k:CHUNK * (k + 1)])
                cc, tt = divmod(k, 2)
                first(2 + g, 2 * b + tt, 2 * h + cc, z_act[g][b][:, HALF * tt + CHUNK * cc:HALF * tt + CHUNK * (cc + 1)])

        h_bf = [[new("h_bf%d_%d" % (q, h), [P, 2, HALF, PACK], BF16) for h in range(2)] for q in range(2)]
        h_rows = [[new("h_rows%d_%d" % (g, h), [P, PACK, HALF], BF16) for h in range(2)] for g in range(2)]

        def hidden_dve(c, g):
            h, b = divmod(c, 2)
            nc.vector.scalar_tensor_tensor(
                out=h_bf[0][h][:, g, CHUNK * b:CHUNK * (b + 1), :],
                in0=z_dve[g][:].rearrange("p (t n) -> p n t", t=PACK),
                scalar=0.0,
                in1=hs_sb[:, g, 0:PACK].unsqueeze(1).to_broadcast([P, CHUNK, PACK]),
                op0=ALU.max, op1=ALU.mult)

        def hidden_act(c, g):
            h, b = divmod(c, 2)
            for tt in range(2):
                t = 2 * b + tt
                nc.scalar.activation(
                    out=h_rows[g][h][:, t, :], in_=z_act[g][b][:, HALF * tt:HALF * (tt + 1)],
                    func=ACT.Relu, scale=hs_abs[:, g, t:t + 1])

        def interleave_h(copy, g, h):
            copy(out=as_words(h_bf[1][h][:, g, :, :]), in_=as_rows(h_rows[g][h][:]))

        def quantize_h(q, h, g0, g1):
            return quantize("h_%d_%d_%d" % (q, h, g0), h_bf[q][h][:, g0:g1, :, :].rearrange("p g n t -> p (g n t)"), (g1 - g0) * HALF)

        w2_bf = new("w2_bf", [P, G, M, PACK], BF16)

        def w2_rows_of(g):
            return w2_raw[g // 2][:, g % 2, :].rearrange("p (t m) -> p t m", t=PACK)

        def interleave_w2(copy, g):
            copy(out=as_words(w2_bf[:, g, :, :]), in_=as_rows(w2_rows_of(g)))

        w2_plain = new("w2_plain", [P, 2, M, PACK], BF16)

        def interleave_w2_pool(dst, g):
            nc.gpsimd.tensor_scalar(
                out=dst, in0=w2_rows_of(g).rearrange("p t m -> p m t"),
                scalar1=1.0, scalar2=0.0, op0=ALU.mult, op1=ALU.add)

        def signed_w2():
            nc.vector.tensor_tensor(
                out=w2_bf[:, 2:4, :, :], in0=w2_plain[:],
                in1=hs_sign[:].unsqueeze(2).to_broadcast([P, 2, M, PACK]), op=ALU.mult)

        def second(bank, q, h_q, g0, g1):
            for g in range(g0, g1):
                for b in range(2):
                    cols = slice(HALF * (g - g0) + CHUNK * b, HALF * (g - g0) + CHUNK * (b + 1))
                    nc.tensor.matmul_mx(
                        out=y_ps[bank][:, cols],
                        lhsT=w2_q[0][:, M * (2 * q + g):M * (2 * q + g + 1)].bitcast(FP8X4),
                        lhsT_scale=w2_q[1][:, M * (2 * q + g):M * (2 * q + g + 1)],
                        rhs=h_q[0][:, cols].bitcast(FP8X4), rhs_scale=h_q[1][:, cols],
                        start=True, stop=True)

        def finish(bank, q, h, g0, g1):
            res = new("res%d_%d_%d" % (q, h, g0), [P, g1 - g0, HALF], F32)
            cols = slice(HALF * h, HALF * (h + 1))
            nc.vector.tensor_tensor(
                out=res[:], in0=y_ps[bank][:, 0:HALF * (g1 - g0)].rearrange("p (g n) -> p g n", n=HALF),
                in1=r_sb[q][:, g0:g1, cols], op=ALU.add)
            nc.sync.dma_start(out=out_rows[:, 2 * q + g0:2 * q + g1, cols], in_=res[:])

        step(0, 0)
        step(0, 1)
        x_bf1 = new("x_bf_h1", [P, HALF, PACK], BF16)
        nc.scalar.copy(out=as_words(x_bf1[:, 0:CHUNK, :]), in_=as_rows(x_raw[1][:, :, 0:CHUNK]))
        nc.vector.tensor_copy(out=as_words(x_bf1[:, CHUNK:HALF, :]), in_=as_rows(x_raw[1][:, :, CHUNK:HALF]))
        nc.scalar.activation(out=hs_abs[:], in_=hs_sb[:, 2:4, 0:PACK], func=ACT.Abs)
        nc.scalar.activation(out=hs_sign[:], in_=hs_sb[:, 2:4, 0:PACK], func=ACT.Sign)
        codes, scales = quantize("x_h1", x_bf1[:].rearrange("p n j -> p (n j)"), HALF)
        x_q[2] = (codes, scales, 0)
        x_q[3] = (codes, scales, CHUNK)
        interleave_w2_pool(w2_plain[:, 0, :, :], 2)
        interleave_w2_pool(w2_plain[:, 1, :, :], 3)
        interleave_w2_pool(w2_bf[:, 1, :, :], 1)
        hidden_dve(0, 0)
        hidden_act(0, 0)
        step(1, 0)
        hidden_dve(0, 1)
        hidden_act(0, 1)
        step(1, 1)
        interleave_w2(nc.scalar.copy, 0)
        hidden_dve(1, 0)
        hidden_act(1, 0)
        step(2, 0)
        hidden_dve(1, 1)
        hidden_act(1, 1)
        step(2, 1)
        signed_w2()
        h_q = quantize_h(0, 0, 0, 2)
        w2_q = quantize("w2", w2_bf[:].rearrange("p g m t -> p (g m t)"), G * M)
        interleave_h(nc.scalar.copy, 0, 0)
        interleave_h(nc.scalar.copy, 1, 0)
        hidden_dve(2, 0)
        second(0, 0, h_q, 0, 2)
        step(3, 0)
        hidden_dve(2, 1)
        hidden_act(2, 0)
        hidden_act(2, 1)
        step(3, 1)
        finish(0, 0, 0, 0, 2)
        h_q = quantize_h(1, 0, 0, 2)
        hidden_dve(3, 0)
        second(1, 1, h_q, 0, 2)
        hidden_dve(3, 1)
        hidden_act(3, 0)
        hidden_act(3, 1)
        h_q = quantize_h(0, 1, 0, 1)
        second(0, 0, h_q, 0, 1)
        finish(1, 1, 0, 0, 2)
        h_q = quantize_h(0, 1, 1, 2)
        second(1, 0, h_q, 1, 2)
        interleave_h(nc.scalar.copy, 0, 1)
        interleave_h(nc.scalar.copy, 1, 1)
        h_q = quantize_h(1, 1, 0, 1)
        finish(0, 0, 1, 0, 1)
        second(0, 1, h_q, 0, 1)
        finish(1, 0, 1, 1, 2)
        h_q = quantize_h(1, 1, 1, 2)
        second(1, 1, h_q, 1, 2)
        finish(0, 1, 1, 0, 1)
        finish(1, 1, 1, 1, 2)
